import numpy as np
import ml_dtypes


def mxq(x, axis, fmt="e4m3"):
    dtype, down = {"e4m3": (ml_dtypes.float8_e4m3fn, 7), "e5m2": (ml_dtypes.float8_e5m2, 14)}[fmt]
    v = np.moveaxis(np.asarray(x, np.float32).astype(ml_dtypes.bfloat16).astype(np.float64), axis, -1)
    blocks = v.reshape(v.shape[:-1] + (-1, 32))
    amax = np.abs(blocks).max(-1, keepdims=True)
    byte = np.maximum(np.where(amax > 0, np.frexp(amax)[1] - 1 + 127, 0) - down, 1)
    scale = np.exp2(byte - 127.0)
    codes = (blocks / scale).astype(np.float32).astype(dtype).astype(np.float64)
    return np.moveaxis((codes * scale).reshape(v.shape), -1, axis)


WIDE = False


def mx_kscale(k):
    if not WIDE:
        return np.ones(k)
    levels = np.array([30, -30])
    if k % 512:
        return np.exp2(np.random.permutation(np.resize(levels, k // 32))).repeat(32)
    a = np.empty((k // 512, 16))
    for p in range(k // 512):
        a[p, :8] = np.random.permutation(np.resize(levels, 8))
        for g in range(8):
            far = levels[np.abs(levels - a[p, g]) >= 10]
            a[p, g + 8] = far[np.random.randint(len(far))]
    return np.exp2(a.ravel()).repeat(32)


def f64(x):
    return np.asarray(x).astype(np.float64)


def striped(idx):
    return np.tile(np.asarray(idx).reshape(-1, 16).T, (8, 1)).astype(np.uint16)


def unstriped(offs):
    return offs[:16].T.reshape(-1).astype(np.int64)


E2M1 = np.array([0.0, 0.5, 1.0, 1.5, 2.0, 3.0, 4.0, 6.0, -0.0, -0.5, -1.0, -1.5, -2.0, -3.0, -4.0, -6.0])


def pack_weight(w, fmt):
    k, n = w.shape
    w = f64(np.asarray(w, np.float32).astype(ml_dtypes.bfloat16)).reshape(k // 32, 32, n)
    amax = np.abs(w).max(1)
    if fmt in ("e4m3", "e5m2"):
        byte = np.frexp(amax)[1] - 1 + 127 - (7 if fmt == "e4m3" else 14)
    else:
        mant, ex = np.frexp(amax / 6.0)
        byte = np.where(mant > 0.5, ex, ex - 1) + 127
    byte = np.clip(np.where(amax > 0, byte, 1), 1, 254)
    scaled = (w * np.exp2(127.0 - byte)[:, None, :]).reshape(k, n).astype(np.float32)
    by_word = np.ascontiguousarray(scaled.reshape(k // 512, 128, 4, n).transpose(0, 1, 3, 2))
    if fmt in ("e4m3", "e5m2"):
        words = by_word.astype(ml_dtypes.float8_e4m3fn if fmt == "e4m3" else ml_dtypes.float8_e5m2).view(np.uint8)
    else:
        c = by_word.astype(ml_dtypes.float4_e2m1fn).view(np.uint8) & 0xF
        words = (c[..., 0::2] | (c[..., 1::2] << 4)).reshape(k // 512, 128, 2 * n)
    return np.ascontiguousarray(words), np.ascontiguousarray(byte.astype(np.uint8).reshape(k // 512, 16, n))


def unpack_weight(words, scales, fmt):
    g, _, n = scales.shape
    words = np.ascontiguousarray(words).reshape(g, 128, n, -1)
    if fmt in ("e4m3", "e5m2"):
        vals = words.view(ml_dtypes.float8_e4m3fn if fmt == "e4m3" else ml_dtypes.float8_e5m2).astype(np.float64)
    else:
        nib = np.empty((g, 128, n, 4), np.uint8)
        nib[..., 0::2] = words & 0xF
        nib[..., 1::2] = words >> 4
        vals = E2M1[nib]
    vals = vals * np.repeat(np.exp2(scales.astype(np.float64) - 127.0), 8, axis=1)[..., None]
    return vals.transpose(0, 1, 3, 2).reshape(g * 512, n)


K, T, I, J, N, Z, S, V, C, O = 512, 1024, 512, 256, 256, 1024, 1024, 1024, 512, 256


def setup_inputs():
    n = np.random.standard_normal
    idx = np.random.permutation(T)[:I]
    idx2 = np.random.permutation(Z)[:J]
    idx3 = np.random.permutation(V)[:J]
    idx4 = np.random.permutation(C)[:J]
    idx5 = np.random.permutation(C)[:J]
    idx6 = np.random.permutation(C)[:O]
    idx7 = np.random.permutation(S)[:N]
    fk = mx_kscale(K)
    fi = mx_kscale(I)
    ti = np.ones(T)
    ti[idx] = fi
    xkp = pack_weight(n((K, T)) * 0.3 * fk[:, None] * ti, "e2m1")
    xqp = pack_weight(n((K, Z)) * 0.3 / fk[:, None], "e5m2")
    xrp = pack_weight(n((K, V)) * 0.3 / fk[:, None], "e4m3")
    vsp = pack_weight(n((I, S)) / fi[:, None], "e2m1")
    return {
        "xk_words": xkp[0],
        "xk_scales": xkp[1],
        "xq_words": xqp[0],
        "xq_scales": xqp[1],
        "xr_words": xrp[0],
        "xr_scales": xrp[1],
        "vs_words": vsp[0],
        "vs_scales": vsp[1],
        "offs": striped(idx),
        "offs2": striped(idx2),
        "offs3": striped(idx3),
        "offs4": striped(idx4),
        "offs5": striped(idx5),
        "offs6": striped(idx6),
        "offs7": striped(idx7),
    }


def reference(xk_words, xk_scales, xq_words, xq_scales, xr_words, xr_scales, vs_words, vs_scales, offs, offs2, offs3, offs4, offs5, offs6, offs7):
    idx = unstriped(offs)
    idx2 = unstriped(offs2)
    idx3 = unstriped(offs3)
    idx4 = unstriped(offs4)
    idx5 = unstriped(offs5)
    idx6 = unstriped(offs6)
    idx7 = unstriped(offs7)
    xku = unpack_weight(xk_words, xk_scales, "e2m1")
    xqu = unpack_weight(xq_words, xq_scales, "e5m2")
    xru = unpack_weight(xr_words, xr_scales, "e4m3")
    vsu = unpack_weight(vs_words, vs_scales, "e2m1")
    xkidxg = xku[:, idx]
    xqidx2g = xqu[:, idx2]
    s1 = xkidxg.T @ xqidx2g
    xridx3g = xru[:, idx3]
    s2 = xkidxg.T @ xridx3g
    pw = np.zeros((I, C))
    pw[:, idx4] = s1
    pv = np.zeros((I, C))
    pv[:, idx5] = s2
    pg = pw + pv
    hid = pg[:, idx6]
    vsidx7g = vsu[:, idx7]
    hidq = mxq(hid, 0, "e5m2")
    y = vsidx7g.T @ hidq
    return y

@@ -1,0 +1,174 @@
+from contextlib import ExitStack
+
+import concourse.mybir as mybir
+
+K, T, I, J, N, C, O = 512, 1024, 512, 256, 256, 512, 256
+FLOPS = 2 * K * I * J * 2 + 2 * I * N * O
+
+F32 = mybir.dt.float32
+BF16 = mybir.dt.bfloat16
+I32 = mybir.dt.int32
+U32 = mybir.dt.uint32
+U16 = mybir.dt.uint16
+U8 = mybir.dt.uint8
+E2M1 = mybir.dt.float4_e2m1fn_x4
+E4M3 = mybir.dt.float8_e4m3fn_x4
+E5M2 = mybir.dt.float8_e5m2_x4
+COPY = mybir.ActivationFunctionType.Copy
+ADD = mybir.AluOpType.add
+
+P = 128
+PACK = 4
+HALF = 128
+SPLIT = 96
+
+
+def tile_list_contest_rivals_shared_plain_kernel(
+    tc, xk_words, xk_scales, xq_words, xq_scales, xr_words, xr_scales, vs_words, vs_scales,
+    offs, offs2, offs3, offs4, offs5, offs6, offs7, out,
+):
+    nc = tc.nc
+    with ExitStack() as ctx:
+        lists = ctx.enter_context(tc.tile_pool(name="lists", bufs=1))
+        held = ctx.enter_context(tc.tile_pool(name="held", bufs=1))
+        psum = ctx.enter_context(tc.psum_pool(name="psum", bufs=1))
+
+        def load_list(src, name):
+            tile = lists.tile(list(src.shape), U16, name=name)
+            nc.sync.dma_start(tile[:], src)
+            return tile
+
+        def load_words(rows, dtype, name):
+            tile = held.tile([P, T], dtype, name=name, align_bytes=64)
+            nc.sync.dma_start(tile[:].bitcast(I32), rows.bitcast(I32))
+            return tile
+
+        def load_scales(scales, name, queue):
+            tile = held.tile([P, T], U8, name=name, align_bytes=64)
+            for q in range(4):
+                rows = scales[0, 4 * q : 4 * q + 4, :].bitcast(I32)
+                queue.dma_start(
+                    tile[32 * q : 32 * q + 32, :].bitcast(I32),
+                    rows.unsqueeze(0).to_broadcast([8, 4, T // 4]),
+                )
+            return tile
+
+        def gather(window, offsets, count, dtype, name):
+            tile = held.tile([P, count], dtype, name=name, align_bytes=64)
+            nc.vector.tensor_copy(tile[:], window[:].indirect(offsets[:]))
+            return tile
+
+        list_k = load_list(offs, "list_k")
+        k_words = load_words(xk_words[0], U16, "k_words")
+        k_scales = load_scales(xk_scales, "k_scales", nc.scalar)
+        list_q = load_list(offs2, "list_q")
+        q_words = load_words(xq_words[0].rearrange("p n t -> p (n t)"), U32, "q_words")
+        q_scales = load_scales(xq_scales, "q_scales", nc.scalar)
+        list_r = load_list(offs3, "list_r")
+        r_words = load_words(xr_words[0].rearrange("p n t -> p (n t)"), U32, "r_words")
+        list_w = load_list(offs4, "list_w")
+        r_scales = load_scales(xr_scales, "r_scales", nc.sync)
+        list_s = load_list(offs7, "list_s")
+        v_words = load_words(vs_words[0], U16, "v_words")
+        list_v = load_list(offs5, "list_v")
+        v_scales = load_scales(vs_scales, "v_scales", nc.sync)
+        list_o = load_list(offs6, "list_o")
+
+        pw = [held.tile([P, C], F32, name="pw%d" % t) for t in range(PACK)]
+        pv = [held.tile([P, C], F32, name="pv%d" % t) for t in range(PACK)]
+        for page in pw + pv:
+            nc.vector.memset(page[:], 0.0)
+
+        kw_listed = gather(k_words, list_k, I, U16, "kw_listed")
+        ks_listed = gather(k_scales, list_k, I, U8, "ks_listed")
+        kw = held.tile([P, I], U16, name="kw", align_bytes=64)
+        ks = held.tile([P, I], U8, name="ks", align_bytes=64)
+        nc.vector.tensor_copy(kw[:].rearrange("p (t m) -> p t m", t=PACK), kw_listed[:].rearrange("p (m t) -> p t m", t=PACK))
+        qw = gather(q_words, list_q, J, U32, "qw")
+        nc.vector.tensor_copy(ks[:].rearrange("p (t m) -> p t m", t=PACK), ks_listed[:].rearrange("p (m t) -> p t m", t=PACK))
+        qs = gather(q_scales, list_q, J, U8, "qs")
+
+        first_s1 = psum.tile([P, J], F32, name="first_s1", tag="first_s1")
+        first_s2 = psum.tile([P, J], F32, name="first_s2", tag="first_s2")
+        both = [psum.tile([P, 2 * J], F32, name="both%d" % t, tag="both%d" % t) for t in range(1, PACK)]
+        s1_sums = [first_s1[:]] + [bank[:, :J] for bank in both]
+        s2_sums = [first_s2[:]] + [bank[:, J:] for bank in both]
+
+        def scores(words, scales, dtype, sums):
+            for t in range(PACK):
+                cols = slice(t * P, (t + 1) * P)
+                nc.tensor.matmul_mx(
+                    out=sums[t], lhsT=kw[:, cols].bitcast(E2M1), lhsT_scale=ks[:, cols],
+                    rhs=words[:].bitcast(dtype), rhs_scale=scales[:], start=True, stop=True,
+                )
+
+        scores(qw, qs, E5M2, s1_sums)
+        rw = gather(r_words, list_r, J, U32, "rw")
+        rs = gather(r_scales, list_r, J, U8, "rs")
+        scores(rw, rs, E4M3, s2_sums)
+
+        def put_s1(t, flat):
+            nc.scalar.activation(pw[t][:].indirect(list_w[:]), flat, COPY)
+
+        def put_s2(t, flat):
+            nc.vector.tensor_copy(pv[t][:].indirect(list_v[:]), flat)
+
+        def add(engine, t, tag):
+            board = held.tile([P, C], F32, name="pg%d" % t, tag=tag)
+            engine.tensor_tensor(board[:], pw[t][:], pv[t][:], ADD)
+            return board
+
+        hid = held.tile([P, PACK, O], F32, name="hid")
+        grouped = held.tile([P, O, PACK], BF16, name="grouped", align_bytes=64)
+
+        s1_0 = held.tile([P, J], F32, name="s1_0")
+        nc.scalar.activation(s1_0[:], first_s1[:], COPY)
+        put_s1(0, s1_0[:])
+        vw = gather(v_words, list_s, N, U16, "vw")
+        s2_0 = held.tile([P, J], F32, name="s2_0")
+        nc.vector.tensor_copy(s2_0[:], first_s2[:])
+        vsc = gather(v_scales, list_s, N, U8, "vsc")
+        put_s2(0, s2_0[:])
+        pg = [add(nc.gpsimd, 0, "pg0")]
+
+        def drain(t):
+            flat = held.tile([P, 2 * J], F32, name="flat%d" % t)
+            nc.scalar.activation(flat[:], both[t - 1][:], COPY)
+            return flat
+
+        ahead = drain(1)
+        for t in range(1, PACK):
+            flat = ahead
+            if t < PACK - 1:
+                ahead = drain(t + 1)
+            put_s1(t, flat[:, :J])
+            put_s2(t, flat[:, J:])
+            if t < PACK - 1:
+                pg.append(add(nc.gpsimd, t, "pg%d" % t))
+        for t in (0, 2):
+            nc.scalar.activation(hid[:, t, :], pg[t][:].indirect(list_o[:]), COPY)
+        nc.vector.tensor_copy(hid[:, 1, :], pg[1][:].indirect(list_o[:]))
+        last = add(nc.vector, 3, "pg1")
+        nc.scalar.activation(hid[:, 3, :HALF], last[:].indirect(list_o[:, : HALF // 16]), COPY)
+        nc.vector.tensor_copy(hid[:, 3, HALF:], last[:].indirect(list_o[:, HALF // 16 :]))
+        nc.scalar.copy(grouped[:, :SPLIT, :], hid[:, :, :SPLIT].rearrange("p t o -> p o t"))
+        nc.vector.tensor_copy(grouped[:, SPLIT:, :], hid[:, :, SPLIT:].rearrange("p t o -> p o t"))
+
+        hw = held.tile([P, O], U32, name="hw", align_bytes=64)
+        hs = held.tile([P, O], U8, name="hs", align_bytes=64)
+        nc.vector.quantize_mx(out=hw[:].bitcast(E5M2), scales=hs[:], in_=grouped[:].rearrange("p o t -> p (o t)"))
+
+        for h in range(N // P):
+            bank = psum.tile([P, O], F32, name="y%d" % h, tag="y%d" % h)
+            cols = slice(h * P, (h + 1) * P)
+            nc.tensor.matmul_mx(
+                out=bank[:], lhsT=vw[:, cols].bitcast(E2M1), lhsT_scale=vsc[:, cols],
+                rhs=hw[:].bitcast(E5M2), rhs_scale=hs[:], start=True, stop=True,
+            )
+            result = held.tile([P, O], F32, name="result%d" % h)
+            if h == 0:
+                nc.scalar.activation(result[:], bank[:], COPY)
+                nc.scalar.dma_start(out[cols, :], result[:])
+            else:
+                nc.vector.tensor_copy(result[:], bank[:])
+                nc.sync.dma_start(out[cols, :], result[:])

@@ -19,8 +19,7 @@ ADD = mybir.AluOpType.add
 
 P = 128
 PACK = 4
-HALF = 128
-SPLIT = 96
+SHARE = 128
 
 
 def tile_list_contest_rivals_shared_plain_kernel(
@@ -43,50 +42,49 @@ def tile_list_contest_rivals_shared_plain_kernel(
             nc.sync.dma_start(tile[:].bitcast(I32), rows.bitcast(I32))
             return tile
 
-        def load_scales(scales, name, queue):
-            tile = held.tile([P, T], U8, name=name, align_bytes=64)
+        def load_scales(tile, scales):
             for q in range(4):
-                rows = scales[0, 4 * q : 4 * q + 4, :].bitcast(I32)
-                queue.dma_start(
-                    tile[32 * q : 32 * q + 32, :].bitcast(I32),
-                    rows.unsqueeze(0).to_broadcast([8, 4, T // 4]),
-                )
-            return tile
+                nc.sync.dma_start(
+                    tile[32 * q : 32 * q + 4, :].bitcast(I32), scales[0, 4 * q : 4 * q + 4, :].bitcast(I32))
 
         def gather(window, offsets, count, dtype, name):
             tile = held.tile([P, count], dtype, name=name, align_bytes=64)
             nc.vector.tensor_copy(tile[:], window[:].indirect(offsets[:]))
             return tile
 
+        k_scales, q_scales, r_scales, v_scales = [
+            held.tile([P, T], U8, name=name, align_bytes=64) for name in ("k_scales", "q_scales", "r_scales", "v_scales")
+        ]
+        pw = [held.tile([P, C], F32, name="pw%d" % t) for t in range(PACK)]
+        pv = [held.tile([P, C], F32, name="pv%d" % t) for t in range(PACK)]
+        for tile in [k_scales, q_scales, r_scales, v_scales] + pw + pv:
+            nc.vector.memset(tile[:].bitcast(I32), 0)
+
         list_k = load_list(offs, "list_k")
         k_words = load_words(xk_words[0], U16, "k_words")
-        k_scales = load_scales(xk_scales, "k_scales", nc.scalar)
         list_q = load_list(offs2, "list_q")
         q_words = load_words(xq_words[0].rearrange("p n t -> p (n t)"), U32, "q_words")
-        q_scales = load_scales(xq_scales, "q_scales", nc.scalar)
+        load_scales(k_scales, xk_scales)
+        load_scales(q_scales, xq_scales)
         list_r = load_list(offs3, "list_r")
         r_words = load_words(xr_words[0].rearrange("p n t -> p (n t)"), U32, "r_words")
+        load_scales(r_scales, xr_scales)
         list_w = load_list(offs4, "list_w")
-        r_scales = load_scales(xr_scales, "r_scales", nc.sync)
         list_s = load_list(offs7, "list_s")
         v_words = load_words(vs_words[0], U16, "v_words")
         list_v = load_list(offs5, "list_v")
-        v_scales = load_scales(vs_scales, "v_scales", nc.sync)
+        load_scales(v_scales, vs_scales)
         list_o = load_list(offs6, "list_o")
 
-        pw = [held.tile([P, C], F32, name="pw%d" % t) for t in range(PACK)]
-        pv = [held.tile([P, C], F32, name="pv%d" % t) for t in range(PACK)]
-        for page in pw + pv:
-            nc.vector.memset(page[:], 0.0)
-
         kw_listed = gather(k_words, list_k, I, U16, "kw_listed")
-        ks_listed = gather(k_scales, list_k, I, U8, "ks_listed")
-        kw = held.tile([P, I], U16, name="kw", align_bytes=64)
-        ks = held.tile([P, I], U8, name="ks", align_bytes=64)
-        nc.vector.tensor_copy(kw[:].rearrange("p (t m) -> p t m", t=PACK), kw_listed[:].rearrange("p (m t) -> p t m", t=PACK))
         qw = gather(q_words, list_q, J, U32, "qw")
-        nc.vector.tensor_copy(ks[:].rearrange("p (t m) -> p t m", t=PACK), ks_listed[:].rearrange("p (m t) -> p t m", t=PACK))
+        kw = held.tile([P, I], U16, name="kw", align_bytes=64)
+        nc.vector.tensor_copy(kw[:].rearrange("p (t m) -> p t m", t=PACK), kw_listed[:].rearrange("p (m t) -> p t m", t=PACK))
+        ks = held.tile([P, I], U8, name="ks", align_bytes=64)
+        nc.vector.tensor_copy(ks[:].rearrange("p (t m) -> p m t", t=PACK), k_scales[:].indirect(list_k[:]))
         qs = gather(q_scales, list_q, J, U8, "qs")
+        rw = gather(r_words, list_r, J, U32, "rw")
+        rs = gather(r_scales, list_r, J, U8, "rs")
 
         first_s1 = psum.tile([P, J], F32, name="first_s1", tag="first_s1")
         first_s2 = psum.tile([P, J], F32, name="first_s2", tag="first_s2")
@@ -94,81 +92,80 @@ def tile_list_contest_rivals_shared_plain_kernel(
         s1_sums = [first_s1[:]] + [bank[:, :J] for bank in both]
         s2_sums = [first_s2[:]] + [bank[:, J:] for bank in both]
 
-        def scores(words, scales, dtype, sums):
-            for t in range(PACK):
-                cols = slice(t * P, (t + 1) * P)
+        for t in range(PACK):
+            cols = slice(t * P, (t + 1) * P)
+            for sums, words, scales in ((s1_sums, qw[:].bitcast(E5M2), qs), (s2_sums, rw[:].bitcast(E4M3), rs)):
                 nc.tensor.matmul_mx(
                     out=sums[t], lhsT=kw[:, cols].bitcast(E2M1), lhsT_scale=ks[:, cols],
-                    rhs=words[:].bitcast(dtype), rhs_scale=scales[:], start=True, stop=True,
+                    rhs=words, rhs_scale=scales[:], start=True, stop=True,
                 )
 
-        scores(qw, qs, E5M2, s1_sums)
-        rw = gather(r_words, list_r, J, U32, "rw")
-        rs = gather(r_scales, list_r, J, U8, "rs")
-        scores(rw, rs, E4M3, s2_sums)
+        def put_scalar(page, offsets, flat):
+            nc.scalar.activation(page[:].indirect(offsets[:]), flat, COPY)
 
-        def put_s1(t, flat):
-            nc.scalar.activation(pw[t][:].indirect(list_w[:]), flat, COPY)
-
-        def put_s2(t, flat):
-            nc.vector.tensor_copy(pv[t][:].indirect(list_v[:]), flat)
+        def put_vector(page, offsets, flat):
+            nc.vector.tensor_copy(page[:].indirect(offsets[:]), flat)
 
         def add(engine, t, tag):
             board = held.tile([P, C], F32, name="pg%d" % t, tag=tag)
             engine.tensor_tensor(board[:], pw[t][:], pv[t][:], ADD)
             return board
 
-        hid = held.tile([P, PACK, O], F32, name="hid")
-        grouped = held.tile([P, O, PACK], BF16, name="grouped", align_bytes=64)
-
-        s1_0 = held.tile([P, J], F32, name="s1_0")
-        nc.scalar.activation(s1_0[:], first_s1[:], COPY)
-        put_s1(0, s1_0[:])
-        vw = gather(v_words, list_s, N, U16, "vw")
-        s2_0 = held.tile([P, J], F32, name="s2_0")
-        nc.vector.tensor_copy(s2_0[:], first_s2[:])
-        vsc = gather(v_scales, list_s, N, U8, "vsc")
-        put_s2(0, s2_0[:])
-        pg = [add(nc.gpsimd, 0, "pg0")]
-
         def drain(t):
             flat = held.tile([P, 2 * J], F32, name="flat%d" % t)
             nc.scalar.activation(flat[:], both[t - 1][:], COPY)
             return flat
 
+        hid = held.tile([P, PACK, O], F32, name="hid")
+
+        s1_0 = held.tile([P, J], F32, name="s1_0")
+        nc.scalar.activation(s1_0[:], first_s1[:], COPY)
+        put_scalar(pw[0], list_w, s1_0[:])
+        vw = gather(v_words, list_s, N, U16, "vw")
+        s2_0 = held.tile([P, J], F32, name="s2_0")
+        nc.vector.tensor_copy(s2_0[:], first_s2[:])
+        put_vector(pv[0], list_v, s2_0[:])
+        pg = [add(nc.gpsimd, 0, "pg0")]
         ahead = drain(1)
         for t in range(1, PACK):
             flat = ahead
             if t < PACK - 1:
                 ahead = drain(t + 1)
-            put_s1(t, flat[:, :J])
-            put_s2(t, flat[:, J:])
+            put_scalar(pw[t], list_w, flat[:, :J])
+            put_vector(pv[t], list_v, flat[:, J:])
             if t < PACK - 1:
                 pg.append(add(nc.gpsimd, t, "pg%d" % t))
-        for t in (0, 2):
+        vsc = gather(v_scales, list_s, N, U8, "vsc")
+        pg.append(add(nc.vector, 3, "pg3"))
+        for t in range(2):
             nc.scalar.activation(hid[:, t, :], pg[t][:].indirect(list_o[:]), COPY)
-        nc.vector.tensor_copy(hid[:, 1, :], pg[1][:].indirect(list_o[:]))
-        last = add(nc.vector, 3, "pg1")
-        nc.scalar.activation(hid[:, 3, :HALF], last[:].indirect(list_o[:, : HALF // 16]), COPY)
-        nc.vector.tensor_copy(hid[:, 3, HALF:], last[:].indirect(list_o[:, HALF // 16 :]))
-        nc.scalar.copy(grouped[:, :SPLIT, :], hid[:, :, :SPLIT].rearrange("p t o -> p o t"))
-        nc.vector.tensor_copy(grouped[:, SPLIT:, :], hid[:, :, SPLIT:].rearrange("p t o -> p o t"))
+        nc.scalar.activation(hid[:, 2, :SHARE], pg[2][:].indirect(list_o[:, : SHARE // 16]), COPY)
+        nc.vector.tensor_copy(hid[:, 2, SHARE:], pg[2][:].indirect(list_o[:, SHARE // 16 :]))
+        nc.vector.tensor_copy(hid[:, 3, :], pg[3][:].indirect(list_o[:]))
 
         hw = held.tile([P, O], U32, name="hw", align_bytes=64)
         hs = held.tile([P, O], U8, name="hs", align_bytes=64)
-        nc.vector.quantize_mx(out=hw[:].bitcast(E5M2), scales=hs[:], in_=grouped[:].rearrange("p o t -> p (o t)"))
-
-        for h in range(N // P):
-            bank = psum.tile([P, O], F32, name="y%d" % h, tag="y%d" % h)
-            cols = slice(h * P, (h + 1) * P)
-            nc.tensor.matmul_mx(
-                out=bank[:], lhsT=vw[:, cols].bitcast(E2M1), lhsT_scale=vsc[:, cols],
-                rhs=hw[:].bitcast(E5M2), rhs_scale=hs[:], start=True, stop=True,
+        halves = [slice(0, O // 2), slice(O // 2, O)]
+        grouped = [held.tile([P, O // 2, PACK], BF16, name="grouped%d" % u, align_bytes=64) for u in range(2)]
+        nc.scalar.copy(grouped[0][:], hid[:, :, halves[0]].rearrange("p t o -> p o t"))
+        nc.vector.tensor_copy(grouped[1][:], hid[:, :, halves[1]].rearrange("p t o -> p o t"))
+        results = [held.tile([P, O], F32, name="result%d" % h) for h in range(N // P)]
+        y_tags = {(0, 1): "y01", (1, 1): "y11", (0, 0): "y00", (1, 0): "first_s1"}
+        for u in (1, 0):
+            nc.vector.quantize_mx(
+                out=hw[:, halves[u]].bitcast(E5M2), scales=hs[:, halves[u]],
+                in_=grouped[u][:].rearrange("p o t -> p (o t)"),
             )
-            result = held.tile([P, O], F32, name="result%d" % h)
-            if h == 0:
-                nc.scalar.activation(result[:], bank[:], COPY)
-                nc.scalar.dma_start(out[cols, :], result[:])
-            else:
-                nc.vector.tensor_copy(result[:], bank[:])
-                nc.sync.dma_start(out[cols, :], result[:])
+            for h in range(N // P):
+                cols = slice(h * P, (h + 1) * P)
+                bank = psum.tile([P, O // 2], F32, name="y%d%d" % (h, u), tag=y_tags[h, u])
+                nc.tensor.matmul_mx(
+                    out=bank[:], lhsT=vw[:, cols].bitcast(E2M1), lhsT_scale=vsc[:, cols],
+                    rhs=hw[:, halves[u]].bitcast(E5M2), rhs_scale=hs[:, halves[u]], start=True, stop=True,
+                )
+                if (h, u) == (1, 0):
+                    nc.vector.tensor_copy(results[h][:, halves[u]], bank[:])
+                else:
+                    nc.scalar.activation(results[h][:, halves[u]], bank[:], COPY)
+        nc.scalar.dma_start(out[:P, :], results[0][:])
+        nc.sync.dma_start(out[P:, :], results[1][:])

@@ -19,7 +19,8 @@ ADD = mybir.AluOpType.add
 
 P = 128
 PACK = 4
-SHARE = 128
+LAST = PACK - 1
+QUADRANTS = 4
 
 
 def tile_list_contest_rivals_shared_plain_kernel(
@@ -43,7 +44,7 @@ def tile_list_contest_rivals_shared_plain_kernel(
             return tile
 
         def load_scales(tile, scales):
-            for q in range(4):
+            for q in range(QUADRANTS):
                 nc.sync.dma_start(
                     tile[32 * q : 32 * q + 4, :].bitcast(I32), scales[0, 4 * q : 4 * q + 4, :].bitcast(I32))
 
@@ -53,10 +54,11 @@ def tile_list_contest_rivals_shared_plain_kernel(
             return tile
 
         k_scales, q_scales, r_scales, v_scales = [
-            held.tile([P, T], U8, name=name, align_bytes=64) for name in ("k_scales", "q_scales", "r_scales", "v_scales")
+            held.tile([P, T], U8, name=name, tag=name, align_bytes=64)
+            for name in ("k_scales", "q_scales", "r_scales", "v_scales")
         ]
         pw = [held.tile([P, C], F32, name="pw%d" % t) for t in range(PACK)]
-        pv = [held.tile([P, C], F32, name="pv%d" % t) for t in range(PACK)]
+        pv = [held.tile([P, C], F32, name="pv%d" % t) for t in range(LAST)]
         for tile in [k_scales, q_scales, r_scales, v_scales] + pw + pv:
             nc.vector.memset(tile[:].bitcast(I32), 0)
 
@@ -69,79 +71,86 @@ def tile_list_contest_rivals_shared_plain_kernel(
         list_r = load_list(offs3, "list_r")
         r_words = load_words(xr_words[0].rearrange("p n t -> p (n t)"), U32, "r_words")
         load_scales(r_scales, xr_scales)
-        list_w = load_list(offs4, "list_w")
-        list_s = load_list(offs7, "list_s")
+        list_pw = load_list(offs4, "list_pw")
+        list_v = load_list(offs7, "list_v")
         v_words = load_words(vs_words[0], U16, "v_words")
-        list_v = load_list(offs5, "list_v")
+        list_pv = load_list(offs5, "list_pv")
         load_scales(v_scales, vs_scales)
-        list_o = load_list(offs6, "list_o")
+        list_pg = load_list(offs6, "list_pg")
+
+        kw = held.tile([P, PACK, P], U16, name="kw", align_bytes=64)
+        ks = held.tile([P, PACK, P], U8, name="ks", align_bytes=64)
+        early_planes, late_planes = slice(0, PACK // 2), slice(PACK // 2, PACK)
+
+        def deal(dealt, listed, planes):
+            nc.vector.tensor_copy(dealt[:, planes, :], listed[:].rearrange("p (m t) -> p t m", t=PACK)[:, planes, :])
 
         kw_listed = gather(k_words, list_k, I, U16, "kw_listed")
+        ks_listed = gather(k_scales, list_k, I, U8, "ks_listed")
+        deal(kw, kw_listed, early_planes)
         qw = gather(q_words, list_q, J, U32, "qw")
-        kw = held.tile([P, I], U16, name="kw", align_bytes=64)
-        nc.vector.tensor_copy(kw[:].rearrange("p (t m) -> p t m", t=PACK), kw_listed[:].rearrange("p (m t) -> p t m", t=PACK))
-        ks = held.tile([P, I], U8, name="ks", align_bytes=64)
-        nc.vector.tensor_copy(ks[:].rearrange("p (t m) -> p m t", t=PACK), k_scales[:].indirect(list_k[:]))
         qs = gather(q_scales, list_q, J, U8, "qs")
+        deal(ks, ks_listed, early_planes)
         rw = gather(r_words, list_r, J, U32, "rw")
         rs = gather(r_scales, list_r, J, U8, "rs")
+        deal(kw, kw_listed, late_planes)
+        deal(ks, ks_listed, late_planes)
+        pv.append(held.tile([P, C], F32, name="pv%d" % LAST, tag="r_scales", align_bytes=64))
+        nc.vector.memset(pv[LAST][:].bitcast(I32), 0)
 
         first_s1 = psum.tile([P, J], F32, name="first_s1", tag="first_s1")
         first_s2 = psum.tile([P, J], F32, name="first_s2", tag="first_s2")
-        both = [psum.tile([P, 2 * J], F32, name="both%d" % t, tag="both%d" % t) for t in range(1, PACK)]
-        s1_sums = [first_s1[:]] + [bank[:, :J] for bank in both]
-        s2_sums = [first_s2[:]] + [bank[:, J:] for bank in both]
+        both = {t: psum.tile([P, 2 * J], F32, name="both%d" % t, tag="both%d" % t) for t in range(1, PACK)}
+        s1_sums = [first_s1[:]] + [both[t][:, :J] for t in range(1, PACK)]
+        s2_sums = [first_s2[:]] + [both[t][:, J:] for t in range(1, PACK)]
 
         for t in range(PACK):
-            cols = slice(t * P, (t + 1) * P)
             for sums, words, scales in ((s1_sums, qw[:].bitcast(E5M2), qs), (s2_sums, rw[:].bitcast(E4M3), rs)):
                 nc.tensor.matmul_mx(
-                    out=sums[t], lhsT=kw[:, cols].bitcast(E2M1), lhsT_scale=ks[:, cols],
+                    out=sums[t], lhsT=kw[:, t, :].bitcast(E2M1), lhsT_scale=ks[:, t, :],
                     rhs=words, rhs_scale=scales[:], start=True, stop=True,
                 )
 
-        def put_scalar(page, offsets, flat):
-            nc.scalar.activation(page[:].indirect(offsets[:]), flat, COPY)
+        def put_s1(t, flat):
+            nc.scalar.activation(pw[t][:].indirect(list_pw[:]), flat, COPY)
 
-        def put_vector(page, offsets, flat):
-            nc.vector.tensor_copy(page[:].indirect(offsets[:]), flat)
+        def put_s2(t, flat):
+            nc.vector.tensor_copy(pv[t][:].indirect(list_pv[:]), flat)
 
-        def add(engine, t, tag):
-            board = held.tile([P, C], F32, name="pg%d" % t, tag=tag)
+        def add(engine, t):
+            board = held.tile([P, C], F32, name="pg%d" % t)
             engine.tensor_tensor(board[:], pw[t][:], pv[t][:], ADD)
             return board
 
         def drain(t):
             flat = held.tile([P, 2 * J], F32, name="flat%d" % t)
-            nc.scalar.activation(flat[:], both[t - 1][:], COPY)
+            nc.scalar.activation(flat[:], both[t][:], COPY)
             return flat
 
         hid = held.tile([P, PACK, O], F32, name="hid")
 
         s1_0 = held.tile([P, J], F32, name="s1_0")
         nc.scalar.activation(s1_0[:], first_s1[:], COPY)
-        put_scalar(pw[0], list_w, s1_0[:])
-        vw = gather(v_words, list_s, N, U16, "vw")
+        put_s1(0, s1_0[:])
         s2_0 = held.tile([P, J], F32, name="s2_0")
         nc.vector.tensor_copy(s2_0[:], first_s2[:])
-        put_vector(pv[0], list_v, s2_0[:])
-        pg = [add(nc.gpsimd, 0, "pg0")]
+        vw = gather(v_words, list_v, N, U16, "vw")
+        put_s2(0, s2_0[:])
+        pg = [add(nc.gpsimd, 0)]
         ahead = drain(1)
         for t in range(1, PACK):
             flat = ahead
-            if t < PACK - 1:
+            if t < LAST:
                 ahead = drain(t + 1)
-            put_scalar(pw[t], list_w, flat[:, :J])
-            put_vector(pv[t], list_v, flat[:, J:])
-            if t < PACK - 1:
-                pg.append(add(nc.gpsimd, t, "pg%d" % t))
-        vsc = gather(v_scales, list_s, N, U8, "vsc")
-        pg.append(add(nc.vector, 3, "pg3"))
-        for t in range(2):
-            nc.scalar.activation(hid[:, t, :], pg[t][:].indirect(list_o[:]), COPY)
-        nc.scalar.activation(hid[:, 2, :SHARE], pg[2][:].indirect(list_o[:, : SHARE // 16]), COPY)
-        nc.vector.tensor_copy(hid[:, 2, SHARE:], pg[2][:].indirect(list_o[:, SHARE // 16 :]))
-        nc.vector.tensor_copy(hid[:, 3, :], pg[3][:].indirect(list_o[:]))
+            put_s1(t, flat[:, :J])
+            put_s2(t, flat[:, J:])
+            if t < LAST:
+                pg.append(add(nc.gpsimd, t))
+        pg.append(add(nc.vector, LAST))
+        vsc = gather(v_scales, list_v, N, U8, "vsc")
+        for t in range(LAST):
+            nc.scalar.activation(hid[:, t, :], pg[t][:].indirect(list_pg[:]), COPY)
+        nc.vector.tensor_copy(hid[:, LAST, :], pg[LAST][:].indirect(list_pg[:]))
 
         hw = held.tile([P, O], U32, name="hw", align_bytes=64)
         hs = held.tile([P, O], U8, name="hs", align_bytes=64)
@@ -149,8 +158,9 @@ def tile_list_contest_rivals_shared_plain_kernel(
         grouped = [held.tile([P, O // 2, PACK], BF16, name="grouped%d" % u, align_bytes=64) for u in range(2)]
         nc.scalar.copy(grouped[0][:], hid[:, :, halves[0]].rearrange("p t o -> p o t"))
         nc.vector.tensor_copy(grouped[1][:], hid[:, :, halves[1]].rearrange("p t o -> p o t"))
+
         results = [held.tile([P, O], F32, name="result%d" % h) for h in range(N // P)]
-        y_tags = {(0, 1): "y01", (1, 1): "y11", (0, 0): "y00", (1, 0): "first_s1"}
+        last_block = (N // P - 1, 0)
         for u in (1, 0):
             nc.vector.quantize_mx(
                 out=hw[:, halves[u]].bitcast(E5M2), scales=hs[:, halves[u]],
@@ -158,12 +168,13 @@ def tile_list_contest_rivals_shared_plain_kernel(
             )
             for h in range(N // P):
                 cols = slice(h * P, (h + 1) * P)
-                bank = psum.tile([P, O // 2], F32, name="y%d%d" % (h, u), tag=y_tags[h, u])
+                tag = "first_s1" if (h, u) == last_block else "y%d%d" % (h, u)
+                bank = psum.tile([P, O // 2], F32, name="y%d%d" % (h, u), tag=tag)
                 nc.tensor.matmul_mx(
                     out=bank[:], lhsT=vw[:, cols].bitcast(E2M1), lhsT_scale=vsc[:, cols],
                     rhs=hw[:, halves[u]].bitcast(E5M2), rhs_scale=hs[:, halves[u]], start=True, stop=True,
                 )
-                if (h, u) == (1, 0):
+                if (h, u) == last_block:
                     nc.vector.tensor_copy(results[h][:, halves[u]], bank[:])
                 else:
                     nc.scalar.activation(results[h][:, halves[u]], bank[:], COPY)

from contextlib import ExitStack

import concourse.mybir as mybir

K, T, I, J, N, C, O = 512, 1024, 512, 256, 256, 512, 256
FLOPS = 2 * K * I * J * 2 + 2 * I * N * O

F32 = mybir.dt.float32
BF16 = mybir.dt.bfloat16
I32 = mybir.dt.int32
U32 = mybir.dt.uint32
U16 = mybir.dt.uint16
U8 = mybir.dt.uint8
E2M1 = mybir.dt.float4_e2m1fn_x4
E4M3 = mybir.dt.float8_e4m3fn_x4
E5M2 = mybir.dt.float8_e5m2_x4
COPY = mybir.ActivationFunctionType.Copy
ADD = mybir.AluOpType.add

P = 128
PACK = 4
LAST = PACK - 1
QUADRANTS = 4


def tile_list_contest_rivals_shared_plain_kernel(
    tc, xk_words, xk_scales, xq_words, xq_scales, xr_words, xr_scales, vs_words, vs_scales,
    offs, offs2, offs3, offs4, offs5, offs6, offs7, out,
):
    nc = tc.nc
    with ExitStack() as ctx:
        lists = ctx.enter_context(tc.tile_pool(name="lists", bufs=1))
        held = ctx.enter_context(tc.tile_pool(name="held", bufs=1))
        psum = ctx.enter_context(tc.psum_pool(name="psum", bufs=1))

        def load_list(src, name):
            tile = lists.tile(list(src.shape), U16, name=name)
            nc.sync.dma_start(tile[:], src)
            return tile

        def load_words(rows, dtype, name):
            tile = held.tile([P, T], dtype, name=name, align_bytes=64)
            nc.sync.dma_start(tile[:].bitcast(I32), rows.bitcast(I32))
            return tile

        def load_scales(tile, scales):
            for q in range(QUADRANTS):
                nc.sync.dma_start(
                    tile[32 * q : 32 * q + 4, :].bitcast(I32), scales[0, 4 * q : 4 * q + 4, :].bitcast(I32))

        def gather(window, offsets, count, dtype, name):
            tile = held.tile([P, count], dtype, name=name, align_bytes=64)
            nc.vector.tensor_copy(tile[:], window[:].indirect(offsets[:]))
            return tile

        k_scales, q_scales, r_scales, v_scales = [
            held.tile([P, T], U8, name=name, tag=name, align_bytes=64)
            for name in ("k_scales", "q_scales", "r_scales", "v_scales")
        ]
        pw = [held.tile([P, C], F32, name="pw%d" % t) for t in range(PACK)]
        pv = [held.tile([P, C], F32, name="pv%d" % t) for t in range(LAST)]
        for tile in [k_scales, q_scales, r_scales, v_scales] + pw + pv:
            nc.vector.memset(tile[:].bitcast(I32), 0)

        list_k = load_list(offs, "list_k")
        k_words = load_words(xk_words[0], U16, "k_words")
        list_q = load_list(offs2, "list_q")
        q_words = load_words(xq_words[0].rearrange("p n t -> p (n t)"), U32, "q_words")
        load_scales(k_scales, xk_scales)
        load_scales(q_scales, xq_scales)
        list_r = load_list(offs3, "list_r")
        r_words = load_words(xr_words[0].rearrange("p n t -> p (n t)"), U32, "r_words")
        load_scales(r_scales, xr_scales)
        list_pw = load_list(offs4, "list_pw")
        list_v = load_list(offs7, "list_v")
        v_words = load_words(vs_words[0], U16, "v_words")
        list_pv = load_list(offs5, "list_pv")
        load_scales(v_scales, vs_scales)
        list_pg = load_list(offs6, "list_pg")

        kw = held.tile([P, PACK, P], U16, name="kw", align_bytes=64)
        ks = held.tile([P, PACK, P], U8, name="ks", align_bytes=64)
        early_planes, late_planes = slice(0, PACK // 2), slice(PACK // 2, PACK)

        def deal(dealt, listed, planes):
            nc.vector.tensor_copy(dealt[:, planes, :], listed[:].rearrange("p (m t) -> p t m", t=PACK)[:, planes, :])

        kw_listed = gather(k_words, list_k, I, U16, "kw_listed")
        ks_listed = gather(k_scales, list_k, I, U8, "ks_listed")
        deal(kw, kw_listed, early_planes)
        qw = gather(q_words, list_q, J, U32, "qw")
        qs = gather(q_scales, list_q, J, U8, "qs")
        deal(ks, ks_listed, early_planes)
        rw = gather(r_words, list_r, J, U32, "rw")
        rs = gather(r_scales, list_r, J, U8, "rs")
        deal(kw, kw_listed, late_planes)
        deal(ks, ks_listed, late_planes)
        pv.append(held.tile([P, C], F32, name="pv%d" % LAST, tag="r_scales", align_bytes=64))
        nc.vector.memset(pv[LAST][:].bitcast(I32), 0)

        first_s1 = psum.tile([P, J], F32, name="first_s1", tag="first_s1")
        first_s2 = psum.tile([P, J], F32, name="first_s2", tag="first_s2")
        both = {t: psum.tile([P, 2 * J], F32, name="both%d" % t, tag="both%d" % t) for t in range(1, PACK)}
        s1_sums = [first_s1[:]] + [both[t][:, :J] for t in range(1, PACK)]
        s2_sums = [first_s2[:]] + [both[t][:, J:] for t in range(1, PACK)]

        for t in range(PACK):
            for sums, words, scales in ((s1_sums, qw[:].bitcast(E5M2), qs), (s2_sums, rw[:].bitcast(E4M3), rs)):
                nc.tensor.matmul_mx(
                    out=sums[t], lhsT=kw[:, t, :].bitcast(E2M1), lhsT_scale=ks[:, t, :],
                    rhs=words, rhs_scale=scales[:], start=True, stop=True,
                )

        def put_s1(t, flat):
            nc.scalar.activation(pw[t][:].indirect(list_pw[:]), flat, COPY)

        def put_s2(t, flat):
            nc.vector.tensor_copy(pv[t][:].indirect(list_pv[:]), flat)

        def add(engine, t):
            board = held.tile([P, C], F32, name="pg%d" % t)
            engine.tensor_tensor(board[:], pw[t][:], pv[t][:], ADD)
            return board

        def drain(t):
            flat = held.tile([P, 2 * J], F32, name="flat%d" % t)
            nc.scalar.activation(flat[:], both[t][:], COPY)
            return flat

        hid = held.tile([P, PACK, O], F32, name="hid")

        s1_0 = held.tile([P, J], F32, name="s1_0")
        nc.scalar.activation(s1_0[:], first_s1[:], COPY)
        put_s1(0, s1_0[:])
        s2_0 = held.tile([P, J], F32, name="s2_0")
        nc.vector.tensor_copy(s2_0[:], first_s2[:])
        vw = gather(v_words, list_v, N, U16, "vw")
        put_s2(0, s2_0[:])
        pg = [add(nc.gpsimd, 0)]
        ahead = drain(1)
        for t in range(1, PACK):
            flat = ahead
            if t < LAST:
                ahead = drain(t + 1)
            put_s1(t, flat[:, :J])
            put_s2(t, flat[:, J:])
            if t < LAST:
                pg.append(add(nc.gpsimd, t))
        pg.append(add(nc.vector, LAST))
        vsc = gather(v_scales, list_v, N, U8, "vsc")
        for t in range(LAST):
            nc.scalar.activation(hid[:, t, :], pg[t][:].indirect(list_pg[:]), COPY)
        nc.vector.tensor_copy(hid[:, LAST, :], pg[LAST][:].indirect(list_pg[:]))

        hw = held.tile([P, O], U32, name="hw", align_bytes=64)
        hs = held.tile([P, O], U8, name="hs", align_bytes=64)
        halves = [slice(0, O // 2), slice(O // 2, O)]
        grouped = [held.tile([P, O // 2, PACK], BF16, name="grouped%d" % u, align_bytes=64) for u in range(2)]
        nc.scalar.copy(grouped[0][:], hid[:, :, halves[0]].rearrange("p t o -> p o t"))
        nc.vector.tensor_copy(grouped[1][:], hid[:, :, halves[1]].rearrange("p t o -> p o t"))

        results = [held.tile([P, O], F32, name="result%d" % h) for h in range(N // P)]
        last_block = (N // P - 1, 0)
        for u in (1, 0):
            nc.vector.quantize_mx(
                out=hw[:, halves[u]].bitcast(E5M2), scales=hs[:, halves[u]],
                in_=grouped[u][:].rearrange("p o t -> p (o t)"),
            )
            for h in range(N // P):
                cols = slice(h * P, (h + 1) * P)
                tag = "first_s1" if (h, u) == last_block else "y%d%d" % (h, u)
                bank = psum.tile([P, O // 2], F32, name="y%d%d" % (h, u), tag=tag)
                nc.tensor.matmul_mx(
                    out=bank[:], lhsT=vw[:, cols].bitcast(E2M1), lhsT_scale=vsc[:, cols],
                    rhs=hw[:, halves[u]].bitcast(E5M2), rhs_scale=hs[:, halves[u]], start=True, stop=True,
                )
                if (h, u) == last_block:
                    nc.vector.tensor_copy(results[h][:, halves[u]], bank[:])
                else:
                    nc.scalar.activation(results[h][:, halves[u]], bank[:], COPY)
        nc.scalar.dma_start(out[:P, :], results[0][:])
        nc.sync.dma_start(out[P:, :], results[1][:])
